import numpy as np
import ml_dtypes


def mxq(x, axis, fmt="e4m3"):
    dtype, down = {"e4m3": (ml_dtypes.float8_e4m3fn, 7), "e5m2": (ml_dtypes.float8_e5m2, 14)}[fmt]
    v = np.moveaxis(np.asarray(x, np.float32).astype(ml_dtypes.bfloat16).astype(np.float64), axis, -1)
    blocks = v.reshape(v.shape[:-1] + (-1, 32))
    amax = np.abs(blocks).max(-1, keepdims=True)
    byte = np.maximum(np.where(amax > 0, np.frexp(amax)[1] - 1 + 127, 0) - down, 1)
    scale = np.exp2(byte - 127.0)
    codes = (blocks / scale).astype(np.float32).astype(dtype).astype(np.float64)
    return np.moveaxis((codes * scale).reshape(v.shape), -1, axis)


WIDE = False


def mx_kscale(k):
    if not WIDE:
        return np.ones(k)
    levels = np.array([10, -10, 5, -5, 0])
    if k % 512:
        return np.exp2(np.random.permutation(np.resize(levels, k // 32))).repeat(32)
    a = np.empty((k // 512, 16))
    for p in range(k // 512):
        a[p, :8] = np.random.permutation(np.resize(levels, 8))
        for g in range(8):
            far = levels[np.abs(levels - a[p, g]) >= 10]
            a[p, g + 8] = far[np.random.randint(len(far))]
    return np.exp2(a.ravel()).repeat(32)


def f64(x):
    return np.asarray(x).astype(np.float64)


def striped(idx):
    return np.tile(idx.reshape(-1, 16).T, (8, 1)).astype(np.uint16)


def unstriped(offs):
    return offs[:16].T.reshape(-1).astype(np.int64)


def striped8(idx):
    return np.concatenate([x.reshape(-1, 16).T for x in idx]).astype(np.uint16)


def runs(offs, k):
    lists = np.stack([offs[16 * r : 16 * r + 16].T.reshape(-1) for r in range(8)]).astype(np.int64)
    return lists[np.arange(k) % 512 // 64]


def pack_weight(w):
    k, n = w.shape
    w = f64(np.asarray(w, np.float32).astype(ml_dtypes.bfloat16)).reshape(k // 32, 32, n)
    amax = np.abs(w).max(1)
    byte = np.clip(np.where(amax > 0, np.frexp(amax)[1] - 1 + 127 - 7, 1), 1, 254)
    scaled = (w * np.exp2(127.0 - byte)[:, None, :]).reshape(k, n).astype(np.float32)
    words = np.ascontiguousarray(scaled.reshape(k // 512, 128, 4, n).transpose(0, 1, 3, 2)).astype(ml_dtypes.float8_e4m3fn).view(np.uint8)
    return words, np.ascontiguousarray(byte.astype(np.uint8).reshape(k // 512, 16, n))


def unpack_weight(words, scales):
    g, p, n, _ = words.shape
    vals = np.ascontiguousarray(words).view(ml_dtypes.float8_e4m3fn).astype(np.float64) * np.repeat(np.exp2(scales.astype(np.float64) - 127.0), 8, axis=1)[..., None]
    return vals.transpose(0, 1, 3, 2).reshape(g * 512, n)


K, T, S, N, G, H = 512, 2048, 512, 512, 2048, 512


def setup_inputs():
    n = np.random.standard_normal
    s = mx_kscale(K)[:, None]
    u = mx_kscale(S)
    packed_xT = pack_weight(n((K, T)) * s)
    packed_dT = pack_weight(n((K, G)) / s)
    return {
        "x_words": packed_xT[0],
        "x_scales": packed_xT[1],
        "d_words": packed_dT[0],
        "d_scales": packed_dT[1],
        "gn": (np.random.uniform(0.5, 1.5, (H, 1)) * u[:, None]).astype(np.float32),
        "w1": (n((H, N)) / np.sqrt(H) / u[:, None]).astype(np.float32),
        "offs": striped8(np.random.randint(0, T, (8, S))),
        "k1": striped8(np.random.randint(0, G, (8, H))),
        "n1": striped(np.random.permutation(S)),
        "n2": striped(np.random.permutation(S)),
        "n3": striped(np.random.permutation(S)),
        "n4": striped(np.random.permutation(S)),
    }


def reference(x_words, x_scales, d_words, d_scales, gn, w1, offs, k1, n1, n2, n3, n4):
    d_k1 = unpack_weight(d_words, d_scales)[np.arange(K)[:, None], runs(k1, K)]
    xq = unpack_weight(x_words, x_scales)[np.arange(K)[:, None], runs(offs, K)]
    h = 0.0625 * (d_k1.T @ xq)
    st = h - h[:, unstriped(n1)]
    z = f64(gn) * (np.maximum(st, st[:, unstriped(n2)]))
    h2 = mxq(f64(w1), 0, "e4m3").T @ mxq(z, 0, "e4m3")
    return h2[:, unstriped(n3)] + 0.75 * h2[:, unstriped(n4)]

@@ -1,0 +1,244 @@
+from contextlib import ExitStack
+
+import concourse.mybir as mybir
+
+F32 = mybir.dt.float32
+BF16 = mybir.dt.bfloat16
+I32 = mybir.dt.int32
+U32 = mybir.dt.uint32
+U16 = mybir.dt.uint16
+U8 = mybir.dt.uint8
+FP8X4 = mybir.dt.float8_e4m3fn_x4
+ALU = mybir.AluOpType
+ACT = mybir.ActivationFunctionType
+
+P = 128
+TABLE = 2048
+S = 512
+HALF = 256
+SPARE = 8
+PIECES = (256, 128, 128)
+FLOPS = 2 * 2 * 512 * 512 * 512
+
+
+def tile_picked_hpqhopmxsum_none_p_kernel(
+    tc, x_words, x_scales, d_words, d_scales, gn, w1, offs, k1, n1, n2, n3, n4, out
+):
+    nc = tc.nc
+    with ExitStack() as ctx:
+        keep = ctx.enter_context(tc.tile_pool(name="keep", bufs=1))
+        psum = ctx.enter_context(tc.psum_pool(name="psum", bufs=1))
+
+        def load_list(name, src):
+            tile = keep.tile([P, S // 16], U16, name=name)
+            nc.sync.dma_start(tile[:], src)
+            return tile
+
+        def load_bytes(name, src):
+            tile = keep.tile([P, TABLE], U8, name=name, align_bytes=64)
+            nc.sync.dma_start(
+                out=tile[:].bitcast(I32), in_=src[0].bitcast(I32).unsqueeze(1).to_broadcast([16, 8, TABLE // 4])
+            )
+            return tile
+
+        def load_words(name, src):
+            tile = keep.tile([P, TABLE], I32, name=name, align_bytes=64)
+            nc.sync.dma_start(out=tile[:], in_=src[0].rearrange("p n t -> p (n t)").bitcast(I32))
+            return tile
+
+        k1_list = load_list("k1_list", k1)
+        d_byte_table = load_bytes("d_byte_table", d_scales)
+        offs_list = load_list("offs_list", offs)
+        x_byte_table = load_bytes("x_byte_table", x_scales)
+        d_word_table = load_words("d_word_table", d_words)
+        n1_list = load_list("n1_list", n1)
+        n2_list = load_list("n2_list", n2)
+        x_word_table = load_words("x_word_table", x_words)
+        gain = keep.tile([P, 4], F32, name="gain")
+        nc.sync.dma_start(out=gain[:], in_=gn.rearrange("(p t) o -> p (t o)", t=4))
+        n3_list = load_list("n3_list", n3)
+        n4_list = load_list("n4_list", n4)
+
+        planes = keep.tile([P, 2 * S], U8, name="planes", align_bytes=64)
+        nc.gpsimd.memset(planes[:].bitcast(I32), 0)
+        h = [keep.tile([P, S + SPARE], F32, name="h%d" % t) for t in range(4)]
+        for tile in h:
+            nc.gpsimd.memset(tile[:, S:], 0.0)
+
+        gain_size = keep.tile([P, 4], F32, name="gain_size")
+        nc.scalar.activation(gain_size[:], gain[:], ACT.Abs, scale=0.0625)
+        negative = keep.tile([P, 4], F32, name="negative")
+        gain_sign = keep.tile([P, 4], F32, name="gain_sign")
+        nc.gpsimd.tensor_scalar(negative[:], gain[:], 0.0, -2.0, ALU.is_lt, ALU.mult)
+        nc.gpsimd.tensor_scalar(gain_sign[:], negative[:], 1.0, 1.0, ALU.mult, ALU.add)
+
+        d_bytes = keep.tile([P, S], U8, name="d_bytes", tag="w_a", align_bytes=64)
+        x_bytes = keep.tile([P, S], U8, name="x_bytes", tag="w_b", align_bytes=64)
+        both = keep.tile([P, 2 * S], U8, name="both", align_bytes=64)
+        nc.vector.tensor_copy(d_bytes[:], d_byte_table[:].indirect(k1_list[:]))
+        nc.vector.tensor_copy(x_bytes[:], x_byte_table[:].indirect(offs_list[:]))
+        nc.vector.tensor_copy(both[:, S:].bitcast(I32), x_bytes[:].bitcast(I32))
+        nc.vector.tensor_copy(
+            both[:, 0:S].rearrange("p (t c i) -> p c t i", t=4, i=16),
+            d_bytes[:].rearrange("p (c i t) -> p c t i", t=4, i=16),
+        )
+        for r in range(4):
+            nc.sync.dma_start(out=planes[r:P:32, :].bitcast(I32), in_=both[8 * r : P : 32, :].bitcast(I32))
+        w_raw = []
+        for a in range(2):
+            tile = keep.tile([P, 4, HALF], F32, name="w_raw%d" % a, tag=("w_a", "w_b")[a], align_bytes=64)
+            nc.sync.dma_start(out=tile[:], in_=w1.rearrange("(p j) n -> p j n", j=4)[:, :, a * HALF : (a + 1) * HALF])
+            w_raw.append(tile)
+
+        d_picked = keep.tile([P, S], U32, name="d_picked", align_bytes=64)
+        d_dealt = keep.tile([P, S], U32, name="d_dealt", align_bytes=64)
+        x_picked = keep.tile([P, S], U32, name="x_picked", align_bytes=64)
+        nc.vector.tensor_copy(d_picked[:], d_word_table[:].bitcast(U32).indirect(k1_list[:]))
+        nc.vector.tensor_copy(
+            d_dealt[:].rearrange("p (t c i) -> p c t i", t=4, i=4),
+            d_picked[:].rearrange("p (c i t) -> p c t i", t=4, i=4),
+        )
+        nc.vector.tensor_copy(x_picked[:], x_word_table[:].bitcast(U32).indirect(offs_list[:]))
+
+        h_banks = [psum.tile([P, S], F32, name="h_bank%d" % t) for t in range(4)]
+        for t in range(4):
+            nc.tensor.matmul_mx(
+                out=h_banks[t][:],
+                lhsT=d_dealt[:, t * P : (t + 1) * P].bitcast(FP8X4),
+                lhsT_scale=planes[:, t * P : (t + 1) * P],
+                rhs=x_picked[:].bitcast(FP8X4),
+                rhs_scale=planes[:, S:],
+                start=True,
+                stop=True,
+            )
+
+        w_codes, w_scales = [], []
+
+        def prepare_w(a):
+            grouped = keep.tile([P, HALF * 4], BF16, name="w_grouped%d" % a, align_bytes=64)
+            nc.vector.tensor_tensor(
+                grouped[:].rearrange("p (c i t) -> p c t i", t=4, i=2),
+                w_raw[a][:].rearrange("p t (c i) -> p c t i", i=2),
+                gain_sign[:].unsqueeze(1).unsqueeze(3).to_broadcast([P, HALF // 2, 4, 2]),
+                ALU.mult,
+            )
+            codes = keep.tile([P, HALF], U32, name="w_codes%d" % a, align_bytes=64)
+            scales = keep.tile([P, HALF], U8, name="w_scales%d" % a, align_bytes=64)
+            nc.vector.quantize_mx(out=codes[:].bitcast(FP8X4), scales=scales[:], in_=grouped[:])
+            w_codes.append(codes)
+            w_scales.append(scales)
+
+        def gather(on_vector, dst, window, offsets, scale=1.0):
+            if on_vector:
+                nc.vector.tensor_copy(dst, window.indirect(offsets))
+            else:
+                nc.scalar.activation(dst, window.indirect(offsets), ACT.Copy, scale=scale)
+
+        def entries(tile, start, width):
+            return tile[:, start // 16 : (start + width) // 16]
+
+        st = keep.tile([P, 4, S], F32, name="st")
+        h_n1 = [keep.tile([P, S], F32, name="h_n1_%d" % t) for t in range(4)]
+        h2 = [keep.tile([P, S], F32, name="h2_%d" % m) for m in range(4)]
+        starts = [sum(PIECES[:a]) for a in range(len(PIECES))]
+        st_n2 = [keep.tile([P, 4, width], F32, name="st_n2_%d" % a) for a, width in enumerate(PIECES)]
+        banks = {}
+
+        def leave_bank(t, on_vector):
+            if on_vector:
+                nc.vector.tensor_scalar(h[t][:, 0:S], h_banks[t][:], gain_size[:, t : t + 1], None, ALU.mult)
+            else:
+                nc.scalar.activation(h[t][:, 0:S], h_banks[t][:], ACT.Copy, scale=gain_size[:, t : t + 1])
+
+        def fetch_n1(t, on_vector):
+            if on_vector:
+                for a in range(2):
+                    gather(True, h_n1[t][:, a * HALF : (a + 1) * HALF], h[t][:], entries(n1_list, a * HALF, HALF))
+            else:
+                gather(False, h_n1[t][:], h[t][:], n1_list[:])
+
+        def fetch_n1_half(t, a, on_vector):
+            gather(on_vector, h_n1[t][:, a * HALF : (a + 1) * HALF], h[t][:], entries(n1_list, a * HALF, HALF))
+
+        def subtract(t):
+            nc.vector.tensor_tensor(st[:, t, :], h[t][:, 0:S], h_n1[t][:], ALU.subtract)
+
+        def fetch_n2(a, t, on_vector):
+            gather(on_vector, st_n2[a][:, t, :], st[:, t, :], entries(n2_list, starts[a], PIECES[a]))
+
+        def second_product(a):
+            start, width = starts[a], PIECES[a]
+            z = keep.tile([P, width * 4], BF16, name="z%d" % a, align_bytes=64)
+            nc.vector.tensor_tensor(
+                z[:].rearrange("p (c i t) -> p c t i", t=4, i=2),
+                st[:, :, start : start + width].rearrange("p t (c i) -> p c t i", i=2),
+                st_n2[a][:].rearrange("p t (c i) -> p c t i", i=2),
+                ALU.max,
+            )
+            z_codes = keep.tile([P, width], U32, name="z_codes%d" % a, align_bytes=64)
+            z_scales = keep.tile([P, width], U8, name="z_scales%d" % a, align_bytes=64)
+            nc.vector.quantize_mx(out=z_codes[:].bitcast(FP8X4), scales=z_scales[:], in_=z[:])
+            per_bank = S // width
+            tiles = [psum.tile([P, per_bank, width], F32, name="h2_bank%d_%d" % (a, b)) for b in range(4 // per_bank)]
+            for m in range(4):
+                w_cols = slice((m % 2) * P, (m % 2 + 1) * P)
+                banks[a, m] = tiles[m // per_bank][:, m % per_bank, :]
+                nc.tensor.matmul_mx(
+                    out=banks[a, m],
+                    lhsT=w_codes[m // 2][:, w_cols].bitcast(FP8X4),
+                    lhsT_scale=w_scales[m // 2][:, w_cols],
+                    rhs=z_codes[:].bitcast(FP8X4),
+                    rhs_scale=z_scales[:],
+                    start=True,
+                    stop=True,
+                )
+
+        def leave_bank2(a, m, on_vector):
+            dst = h2[m][:, starts[a] : starts[a] + PIECES[a]]
+            if on_vector:
+                nc.vector.tensor_copy(dst, banks[a, m])
+            else:
+                nc.scalar.copy(dst, banks[a, m])
+
+        def finish(m, a, form):
+            h2_n4 = keep.tile([P, HALF], F32, name="h2_n4_%d_%d" % (m, a))
+            gather(False, h2_n4[:], h2[m][:], entries(n4_list, a * HALF, HALF), scale=0.75)
+            result = keep.tile([P, HALF], F32, name="result%d_%d" % (m, a))
+            if form == "fused":
+                nc.vector.tensor_tensor(result[:], h2[m][:].indirect(entries(n3_list, a * HALF, HALF)), h2_n4[:], ALU.add)
+            else:
+                h2_n3 = keep.tile([P, HALF], F32, name="h2_n3_%d_%d" % (m, a))
+                gather(form[0] == "v", h2_n3[:], h2[m][:], entries(n3_list, a * HALF, HALF))
+                engine = nc.vector if form[1] == "v" else nc.gpsimd
+                engine.tensor_tensor(result[:], h2_n3[:], h2_n4[:], ALU.add)
+            nc.sync.dma_start(out=out[m * P : (m + 1) * P, a * HALF : (a + 1) * HALF], in_=result[:])
+
+        prepare_w(0)
+        leave_bank(0, False)
+        leave_bank(1, True)
+        fetch_n1(0, False)
+        fetch_n1(1, True)
+        leave_bank(2, False)
+        leave_bank(3, False)
+        subtract(0)
+        subtract(1)
+        fetch_n1(2, False)
+        fetch_n1(3, True)
+        fetch_n2(0, 0, False)
+        fetch_n2(0, 1, False)
+        subtract(2)
+        subtract(3)
+        fetch_n2(0, 2, False)
+        fetch_n2(0, 3, False)
+        prepare_w(1)
+        for a in range(1, 3):
+            for t in range(4):
+                fetch_n2(a, t, False)
+        for a in range(3):
+            second_product(a)
+        for a in range(3):
+            for m in range(4):
+                leave_bank2(a, m, a == 2 and m > 0)
+        for m in range(4):
+            for a in range(2):
+                finish(m, a, "fused")

@@ -50,12 +50,15 @@ def tile_picked_hpqhopmxsum_none_p_kernel(
         d_byte_table = load_bytes("d_byte_table", d_scales)
         offs_list = load_list("offs_list", offs)
         x_byte_table = load_bytes("x_byte_table", x_scales)
+        gain = keep.tile([P, 4], F32, name="gain")
+        nc.sync.dma_start(out=gain[:], in_=gn.rearrange("(p t) o -> p (t o)", t=4))
+        w_rows = w1.rearrange("(p j) n -> p j n", j=4)
+        w_raw0 = keep.tile([P, 4, HALF], F32, name="w_raw0")
+        nc.sync.dma_start(out=w_raw0[:], in_=w_rows[:, :, 0:HALF])
         d_word_table = load_words("d_word_table", d_words)
         n1_list = load_list("n1_list", n1)
         n2_list = load_list("n2_list", n2)
         x_word_table = load_words("x_word_table", x_words)
-        gain = keep.tile([P, 4], F32, name="gain")
-        nc.sync.dma_start(out=gain[:], in_=gn.rearrange("(p t) o -> p (t o)", t=4))
         n3_list = load_list("n3_list", n3)
         n4_list = load_list("n4_list", n4)
 
@@ -73,7 +76,7 @@ def tile_picked_hpqhopmxsum_none_p_kernel(
         nc.gpsimd.tensor_scalar(gain_sign[:], negative[:], 1.0, 1.0, ALU.mult, ALU.add)
 
         d_bytes = keep.tile([P, S], U8, name="d_bytes", tag="w_a", align_bytes=64)
-        x_bytes = keep.tile([P, S], U8, name="x_bytes", tag="w_b", align_bytes=64)
+        x_bytes = keep.tile([P, S], U8, name="x_bytes", align_bytes=64)
         both = keep.tile([P, 2 * S], U8, name="both", align_bytes=64)
         nc.vector.tensor_copy(d_bytes[:], d_byte_table[:].indirect(k1_list[:]))
         nc.vector.tensor_copy(x_bytes[:], x_byte_table[:].indirect(offs_list[:]))
@@ -84,11 +87,34 @@ def tile_picked_hpqhopmxsum_none_p_kernel(
         )
         for r in range(4):
             nc.sync.dma_start(out=planes[r:P:32, :].bitcast(I32), in_=both[8 * r : P : 32, :].bitcast(I32))
-        w_raw = []
-        for a in range(2):
-            tile = keep.tile([P, 4, HALF], F32, name="w_raw%d" % a, tag=("w_a", "w_b")[a], align_bytes=64)
-            nc.sync.dma_start(out=tile[:], in_=w1.rearrange("(p j) n -> p j n", j=4)[:, :, a * HALF : (a + 1) * HALF])
-            w_raw.append(tile)
+        w_raw1 = keep.tile([P, 4, HALF], F32, name="w_raw1", tag="w_a", align_bytes=64)
+        nc.sync.dma_start(out=w_raw1[:], in_=w_rows[:, :, HALF:])
+        w_raw = [w_raw0, w_raw1]
+
+        w_codes, w_scales = [], []
+
+        def prepare_w(a):
+            grouped = keep.tile([P, HALF * 4], BF16, name="w_grouped%d" % a, align_bytes=64)
+            if a == 0:
+                signed = keep.tile([P, 4, HALF], BF16, name="w_signed")
+                for j in range(4):
+                    nc.scalar.activation(signed[:, j, :], w_raw[a][:, j, :], ACT.Copy, scale=gain_sign[:, j : j + 1])
+                nc.scalar.copy(
+                    grouped[:].rearrange("p (c i t) -> p c t i", t=4, i=4),
+                    signed[:].rearrange("p t (c i) -> p c t i", i=4),
+                )
+            else:
+                nc.vector.tensor_tensor(
+                    grouped[:].rearrange("p (c i t) -> p c t i", t=4, i=2),
+                    w_raw[a][:].rearrange("p t (c i) -> p c t i", i=2),
+                    gain_sign[:].unsqueeze(1).unsqueeze(3).to_broadcast([P, HALF // 2, 4, 2]),
+                    ALU.mult,
+                )
+            codes = keep.tile([P, HALF], U32, name="w_codes%d" % a, align_bytes=64)
+            scales = keep.tile([P, HALF], U8, name="w_scales%d" % a, align_bytes=64)
+            nc.vector.quantize_mx(out=codes[:].bitcast(FP8X4), scales=scales[:], in_=grouped[:])
+            w_codes.append(codes)
+            w_scales.append(scales)
 
         d_picked = keep.tile([P, S], U32, name="d_picked", align_bytes=64)
         d_dealt = keep.tile([P, S], U32, name="d_dealt", align_bytes=64)
@@ -98,35 +124,23 @@ def tile_picked_hpqhopmxsum_none_p_kernel(
             d_dealt[:].rearrange("p (t c i) -> p c t i", t=4, i=4),
             d_picked[:].rearrange("p (c i t) -> p c t i", t=4, i=4),
         )
-        nc.vector.tensor_copy(x_picked[:], x_word_table[:].bitcast(U32).indirect(offs_list[:]))
-
+        prepare_w(0)
         h_banks = [psum.tile([P, S], F32, name="h_bank%d" % t) for t in range(4)]
-        for t in range(4):
+        for a in range(2):
+            cols = slice(a * HALF, (a + 1) * HALF)
+            nc.vector.tensor_copy(
+                x_picked[:, cols], x_word_table[:].bitcast(U32).indirect(offs_list[:, a * 16 : (a + 1) * 16])
+            )
+        for t, a in ((0, 0), (1, 0), (0, 1), (1, 1), (2, 0), (2, 1), (3, 0), (3, 1)):
             nc.tensor.matmul_mx(
-                out=h_banks[t][:],
+                out=h_banks[t][:, a * HALF : (a + 1) * HALF],
                 lhsT=d_dealt[:, t * P : (t + 1) * P].bitcast(FP8X4),
                 lhsT_scale=planes[:, t * P : (t + 1) * P],
-                rhs=x_picked[:].bitcast(FP8X4),
-                rhs_scale=planes[:, S:],
+                rhs=x_picked[:, a * HALF : (a + 1) * HALF].bitcast(FP8X4),
+                rhs_scale=planes[:, S + a * HALF : S + (a + 1) * HALF],
                 start=True,
                 stop=True,
             )
-
-        w_codes, w_scales = [], []
-
-        def prepare_w(a):
-            grouped = keep.tile([P, HALF * 4], BF16, name="w_grouped%d" % a, align_bytes=64)
-            nc.vector.tensor_tensor(
-                grouped[:].rearrange("p (c i t) -> p c t i", t=4, i=2),
-                w_raw[a][:].rearrange("p t (c i) -> p c t i", i=2),
-                gain_sign[:].unsqueeze(1).unsqueeze(3).to_broadcast([P, HALF // 2, 4, 2]),
-                ALU.mult,
-            )
-            codes = keep.tile([P, HALF], U32, name="w_codes%d" % a, align_bytes=64)
-            scales = keep.tile([P, HALF], U8, name="w_scales%d" % a, align_bytes=64)
-            nc.vector.quantize_mx(out=codes[:].bitcast(FP8X4), scales=scales[:], in_=grouped[:])
-            w_codes.append(codes)
-            w_scales.append(scales)
 
         def gather(on_vector, dst, window, offsets, scale=1.0):
             if on_vector:
@@ -138,10 +152,10 @@ def tile_picked_hpqhopmxsum_none_p_kernel(
             return tile[:, start // 16 : (start + width) // 16]
 
         st = keep.tile([P, 4, S], F32, name="st")
-        h_n1 = [keep.tile([P, S], F32, name="h_n1_%d" % t) for t in range(4)]
+        h_n1 = [keep.tile([P, S], F32, name="h_n1_%d" % t, tag="fetched%d" % t) for t in range(4)]
         h2 = [keep.tile([P, S], F32, name="h2_%d" % m) for m in range(4)]
         starts = [sum(PIECES[:a]) for a in range(len(PIECES))]
-        st_n2 = [keep.tile([P, 4, width], F32, name="st_n2_%d" % a) for a, width in enumerate(PIECES)]
+        st_n2 = {}
         banks = {}
 
         def leave_bank(t, on_vector):
@@ -164,17 +178,25 @@ def tile_picked_hpqhopmxsum_none_p_kernel(
             nc.vector.tensor_tensor(st[:, t, :], h[t][:, 0:S], h_n1[t][:], ALU.subtract)
 
         def fetch_n2(a, t, on_vector):
+            if a not in st_n2:
+                st_n2[a] = keep.tile([P, 4, PIECES[a]], F32, name="st_n2_%d" % a, tag=("st_n2", "fetched2", "fetched3")[a])
             gather(on_vector, st_n2[a][:, t, :], st[:, t, :], entries(n2_list, starts[a], PIECES[a]))
 
-        def second_product(a):
+        zs = {}
+
+        def larger(a):
             start, width = starts[a], PIECES[a]
             z = keep.tile([P, width * 4], BF16, name="z%d" % a, align_bytes=64)
+            zs[a] = z
             nc.vector.tensor_tensor(
                 z[:].rearrange("p (c i t) -> p c t i", t=4, i=2),
                 st[:, :, start : start + width].rearrange("p t (c i) -> p c t i", i=2),
                 st_n2[a][:].rearrange("p t (c i) -> p c t i", i=2),
                 ALU.max,
             )
+
+        def second_product(a):
+            width, z = PIECES[a], zs[a]
             z_codes = keep.tile([P, width], U32, name="z_codes%d" % a, align_bytes=64)
             z_scales = keep.tile([P, width], U8, name="z_scales%d" % a, align_bytes=64)
             nc.vector.quantize_mx(out=z_codes[:].bitcast(FP8X4), scales=z_scales[:], in_=z[:])
@@ -200,11 +222,19 @@ def tile_picked_hpqhopmxsum_none_p_kernel(
             else:
                 nc.scalar.copy(dst, banks[a, m])
 
+        early = {}
+
+        def fetch_n3(m, a):
+            early[m, a] = keep.tile([P, HALF], F32, name="early_n3_%d_%d" % (m, a))
+            gather(True, early[m, a][:], h2[m][:], entries(n3_list, a * HALF, HALF))
+
         def finish(m, a, form):
             h2_n4 = keep.tile([P, HALF], F32, name="h2_n4_%d_%d" % (m, a))
             gather(False, h2_n4[:], h2[m][:], entries(n4_list, a * HALF, HALF), scale=0.75)
             result = keep.tile([P, HALF], F32, name="result%d_%d" % (m, a))
-            if form == "fused":
+            if form == "early":
+                nc.vector.tensor_tensor(result[:], early[m, a][:], h2_n4[:], ALU.add)
+            elif form == "fused":
                 nc.vector.tensor_tensor(result[:], h2[m][:].indirect(entries(n3_list, a * HALF, HALF)), h2_n4[:], ALU.add)
             else:
                 h2_n3 = keep.tile([P, HALF], F32, name="h2_n3_%d_%d" % (m, a))
@@ -213,32 +243,30 @@ def tile_picked_hpqhopmxsum_none_p_kernel(
                 engine.tensor_tensor(result[:], h2_n3[:], h2_n4[:], ALU.add)
             nc.sync.dma_start(out=out[m * P : (m + 1) * P, a * HALF : (a + 1) * HALF], in_=result[:])
 
-        prepare_w(0)
+        prepare_w(1)
         leave_bank(0, False)
-        leave_bank(1, True)
-        fetch_n1(0, False)
+        leave_bank(1, False)
         fetch_n1(1, True)
+        fetch_n1(0, False)
         leave_bank(2, False)
         leave_bank(3, False)
-        subtract(0)
         subtract(1)
+        subtract(0)
         fetch_n1(2, False)
-        fetch_n1(3, True)
-        fetch_n2(0, 0, False)
-        fetch_n2(0, 1, False)
+        fetch_n1_half(3, 0, True)
+        fetch_n1_half(3, 1, False)
         subtract(2)
         subtract(3)
-        fetch_n2(0, 2, False)
-        fetch_n2(0, 3, False)
-        prepare_w(1)
-        for a in range(1, 3):
-            for t in range(4):
-                fetch_n2(a, t, False)
         for a in range(3):
+            for t in range(4):
+                fetch_n2(a, t, t == 3)
+        for a in range(3):
+            larger(a)
             second_product(a)
         for a in range(3):
             for m in range(4):
                 leave_bank2(a, m, a == 2 and m > 0)
+        fetch_n3(3, 1)
         for m in range(4):
             for a in range(2):
-                finish(m, a, "fused")
+                finish(m, a, "early" if (m, a) == (3, 1) else "fused")

@@ -13,11 +13,14 @@ ALU = mybir.AluOpType
 ACT = mybir.ActivationFunctionType
 
 P = 128
+PACK = 4
 TABLE = 2048
 S = 512
-HALF = 256
+HALF = S // 2
 SPARE = 8
-PIECES = (256, 128, 128)
+VECTOR_TILE = 1
+SHARED_TILE = 3
+N2_VECTOR_TILE = 2
 FLOPS = 2 * 2 * 512 * 512 * 512
 
 
@@ -29,118 +32,27 @@ def tile_picked_hpqhopmxsum_none_p_kernel(
         keep = ctx.enter_context(tc.tile_pool(name="keep", bufs=1))
         psum = ctx.enter_context(tc.psum_pool(name="psum", bufs=1))
 
+        def half(a):
+            return slice(a * HALF, (a + 1) * HALF)
+
+        def half_list(tile, a):
+            return tile[:, a * HALF // 16 : (a + 1) * HALF // 16]
+
         def load_list(name, src):
             tile = keep.tile([P, S // 16], U16, name=name)
             nc.sync.dma_start(tile[:], src)
             return tile
 
-        def load_bytes(name, src):
+        def load_scale_table(name, src):
             tile = keep.tile([P, TABLE], U8, name=name, align_bytes=64)
-            nc.sync.dma_start(
-                out=tile[:].bitcast(I32), in_=src[0].bitcast(I32).unsqueeze(1).to_broadcast([16, 8, TABLE // 4])
-            )
+            rows = src[0].bitcast(I32).unsqueeze(1).to_broadcast([16, 8, TABLE // 4])
+            nc.sync.dma_start(out=tile[:].bitcast(I32), in_=rows)
             return tile
 
-        def load_words(name, src):
+        def load_word_table(name, src):
             tile = keep.tile([P, TABLE], I32, name=name, align_bytes=64)
             nc.sync.dma_start(out=tile[:], in_=src[0].rearrange("p n t -> p (n t)").bitcast(I32))
             return tile
-
-        k1_list = load_list("k1_list", k1)
-        d_byte_table = load_bytes("d_byte_table", d_scales)
-        offs_list = load_list("offs_list", offs)
-        x_byte_table = load_bytes("x_byte_table", x_scales)
-        gain = keep.tile([P, 4], F32, name="gain")
-        nc.sync.dma_start(out=gain[:], in_=gn.rearrange("(p t) o -> p (t o)", t=4))
-        w_rows = w1.rearrange("(p j) n -> p j n", j=4)
-        w_raw0 = keep.tile([P, 4, HALF], F32, name="w_raw0")
-        nc.sync.dma_start(out=w_raw0[:], in_=w_rows[:, :, 0:HALF])
-        d_word_table = load_words("d_word_table", d_words)
-        n1_list = load_list("n1_list", n1)
-        n2_list = load_list("n2_list", n2)
-        x_word_table = load_words("x_word_table", x_words)
-        n3_list = load_list("n3_list", n3)
-        n4_list = load_list("n4_list", n4)
-
-        planes = keep.tile([P, 2 * S], U8, name="planes", align_bytes=64)
-        nc.gpsimd.memset(planes[:].bitcast(I32), 0)
-        h = [keep.tile([P, S + SPARE], F32, name="h%d" % t) for t in range(4)]
-        for tile in h:
-            nc.gpsimd.memset(tile[:, S:], 0.0)
-
-        gain_size = keep.tile([P, 4], F32, name="gain_size")
-        nc.scalar.activation(gain_size[:], gain[:], ACT.Abs, scale=0.0625)
-        negative = keep.tile([P, 4], F32, name="negative")
-        gain_sign = keep.tile([P, 4], F32, name="gain_sign")
-        nc.gpsimd.tensor_scalar(negative[:], gain[:], 0.0, -2.0, ALU.is_lt, ALU.mult)
-        nc.gpsimd.tensor_scalar(gain_sign[:], negative[:], 1.0, 1.0, ALU.mult, ALU.add)
-
-        d_bytes = keep.tile([P, S], U8, name="d_bytes", tag="w_a", align_bytes=64)
-        x_bytes = keep.tile([P, S], U8, name="x_bytes", align_bytes=64)
-        both = keep.tile([P, 2 * S], U8, name="both", align_bytes=64)
-        nc.vector.tensor_copy(d_bytes[:], d_byte_table[:].indirect(k1_list[:]))
-        nc.vector.tensor_copy(x_bytes[:], x_byte_table[:].indirect(offs_list[:]))
-        nc.vector.tensor_copy(both[:, S:].bitcast(I32), x_bytes[:].bitcast(I32))
-        nc.vector.tensor_copy(
-            both[:, 0:S].rearrange("p (t c i) -> p c t i", t=4, i=16),
-            d_bytes[:].rearrange("p (c i t) -> p c t i", t=4, i=16),
-        )
-        for r in range(4):
-            nc.sync.dma_start(out=planes[r:P:32, :].bitcast(I32), in_=both[8 * r : P : 32, :].bitcast(I32))
-        w_raw1 = keep.tile([P, 4, HALF], F32, name="w_raw1", tag="w_a", align_bytes=64)
-        nc.sync.dma_start(out=w_raw1[:], in_=w_rows[:, :, HALF:])
-        w_raw = [w_raw0, w_raw1]
-
-        w_codes, w_scales = [], []
-
-        def prepare_w(a):
-            grouped = keep.tile([P, HALF * 4], BF16, name="w_grouped%d" % a, align_bytes=64)
-            if a == 0:
-                signed = keep.tile([P, 4, HALF], BF16, name="w_signed")
-                for j in range(4):
-                    nc.scalar.activation(signed[:, j, :], w_raw[a][:, j, :], ACT.Copy, scale=gain_sign[:, j : j + 1])
-                nc.scalar.copy(
-                    grouped[:].rearrange("p (c i t) -> p c t i", t=4, i=4),
-                    signed[:].rearrange("p t (c i) -> p c t i", i=4),
-                )
-            else:
-                nc.vector.tensor_tensor(
-                    grouped[:].rearrange("p (c i t) -> p c t i", t=4, i=2),
-                    w_raw[a][:].rearrange("p t (c i) -> p c t i", i=2),
-                    gain_sign[:].unsqueeze(1).unsqueeze(3).to_broadcast([P, HALF // 2, 4, 2]),
-                    ALU.mult,
-                )
-            codes = keep.tile([P, HALF], U32, name="w_codes%d" % a, align_bytes=64)
-            scales = keep.tile([P, HALF], U8, name="w_scales%d" % a, align_bytes=64)
-            nc.vector.quantize_mx(out=codes[:].bitcast(FP8X4), scales=scales[:], in_=grouped[:])
-            w_codes.append(codes)
-            w_scales.append(scales)
-
-        d_picked = keep.tile([P, S], U32, name="d_picked", align_bytes=64)
-        d_dealt = keep.tile([P, S], U32, name="d_dealt", align_bytes=64)
-        x_picked = keep.tile([P, S], U32, name="x_picked", align_bytes=64)
-        nc.vector.tensor_copy(d_picked[:], d_word_table[:].bitcast(U32).indirect(k1_list[:]))
-        nc.vector.tensor_copy(
-            d_dealt[:].rearrange("p (t c i) -> p c t i", t=4, i=4),
-            d_picked[:].rearrange("p (c i t) -> p c t i", t=4, i=4),
-        )
-        prepare_w(0)
-        h_banks = [psum.tile([P, S], F32, name="h_bank%d" % t) for t in range(4)]
-        for a in range(2):
-            cols = slice(a * HALF, (a + 1) * HALF)
-            nc.vector.tensor_copy(
-                x_picked[:, cols], x_word_table[:].bitcast(U32).indirect(offs_list[:, a * 16 : (a + 1) * 16])
-            )
-        for t, a in ((0, 0), (1, 0), (0, 1), (1, 1), (2, 0), (2, 1), (3, 0), (3, 1)):
-            nc.tensor.matmul_mx(
-                out=h_banks[t][:, a * HALF : (a + 1) * HALF],
-                lhsT=d_dealt[:, t * P : (t + 1) * P].bitcast(FP8X4),
-                lhsT_scale=planes[:, t * P : (t + 1) * P],
-                rhs=x_picked[:, a * HALF : (a + 1) * HALF].bitcast(FP8X4),
-                rhs_scale=planes[:, S + a * HALF : S + (a + 1) * HALF],
-                start=True,
-                stop=True,
-            )
 
         def gather(on_vector, dst, window, offsets, scale=1.0):
             if on_vector:
@@ -148,125 +60,179 @@ def tile_picked_hpqhopmxsum_none_p_kernel(
             else:
                 nc.scalar.activation(dst, window.indirect(offsets), ACT.Copy, scale=scale)
 
-        def entries(tile, start, width):
-            return tile[:, start // 16 : (start + width) // 16]
+        def quantise(name, grouped):
+            codes = keep.tile([P, HALF], U32, name=name + "_codes", align_bytes=64)
+            scales = keep.tile([P, HALF], U8, name=name + "_scales", align_bytes=64)
+            nc.vector.quantize_mx(out=codes[:].bitcast(FP8X4), scales=scales[:], in_=grouped[:])
+            return codes, scales
 
-        st = keep.tile([P, 4, S], F32, name="st")
-        h_n1 = [keep.tile([P, S], F32, name="h_n1_%d" % t, tag="fetched%d" % t) for t in range(4)]
-        h2 = [keep.tile([P, S], F32, name="h2_%d" % m) for m in range(4)]
-        starts = [sum(PIECES[:a]) for a in range(len(PIECES))]
-        st_n2 = {}
-        banks = {}
+        def product(bank, left_codes, left_scales, right_codes, right_scales):
+            nc.tensor.matmul_mx(
+                out=bank,
+                lhsT=left_codes.bitcast(FP8X4),
+                lhsT_scale=left_scales,
+                rhs=right_codes.bitcast(FP8X4),
+                rhs_scale=right_scales,
+                start=True,
+                stop=True,
+            )
 
-        def leave_bank(t, on_vector):
-            if on_vector:
+        k1_list = load_list("k1_list", k1)
+        d_scale_table = load_scale_table("d_scale_table", d_scales)
+        offs_list = load_list("offs_list", offs)
+        x_scale_table = load_scale_table("x_scale_table", x_scales)
+        gain = keep.tile([P, PACK], F32, name="gain")
+        nc.sync.dma_start(out=gain[:], in_=gn.rearrange("(p t) o -> p (t o)", t=PACK))
+        w_rows = w1.rearrange("(p t) n -> p t n", t=PACK)
+        w_first = keep.tile([P, PACK, HALF], F32, name="w_first")
+        nc.sync.dma_start(out=w_first[:], in_=w_rows[:, :, half(0)])
+        d_word_table = load_word_table("d_word_table", d_words)
+        n1_list = load_list("n1_list", n1)
+        n2_list = load_list("n2_list", n2)
+        x_word_table = load_word_table("x_word_table", x_words)
+        n3_list = load_list("n3_list", n3)
+        n4_list = load_list("n4_list", n4)
+
+        planes = keep.tile([P, 2 * S], U8, name="planes", align_bytes=64)
+        nc.gpsimd.memset(planes[:].bitcast(I32), 0)
+        h = [keep.tile([P, S + SPARE], F32, name="h%d" % t) for t in range(PACK)]
+        for tile in h:
+            nc.gpsimd.memset(tile[:, S:], 0.0)
+
+        gain_size = keep.tile([P, PACK], F32, name="gain_size")
+        nc.scalar.activation(gain_size[:], gain[:], ACT.Abs, scale=0.0625)
+        negative = keep.tile([P, PACK], F32, name="negative")
+        gain_sign = keep.tile([P, PACK], F32, name="gain_sign")
+        nc.gpsimd.tensor_scalar(negative[:], gain[:], 0.0, -2.0, ALU.is_lt, ALU.mult)
+        nc.gpsimd.tensor_scalar(gain_sign[:], negative[:], 1.0, 1.0, ALU.mult, ALU.add)
+
+        d_bytes = keep.tile([P, S], U8, name="d_bytes", tag="bytes_then_w", align_bytes=64)
+        x_bytes = keep.tile([P, S], U8, name="x_bytes", align_bytes=64)
+        both = keep.tile([P, 2 * S], U8, name="both", align_bytes=64)
+        nc.vector.tensor_copy(d_bytes[:], d_scale_table[:].indirect(k1_list[:]))
+        nc.vector.tensor_copy(x_bytes[:], x_scale_table[:].indirect(offs_list[:]))
+        nc.vector.tensor_copy(both[:, S:].bitcast(I32), x_bytes[:].bitcast(I32))
+        nc.vector.tensor_copy(
+            both[:, 0:S].rearrange("p (t c i) -> p c t i", t=PACK, i=16),
+            d_bytes[:].rearrange("p (c i t) -> p c t i", t=PACK, i=16),
+        )
+        for r in range(4):
+            nc.sync.dma_start(out=planes[r:P:32, :].bitcast(I32), in_=both[8 * r : P : 32, :].bitcast(I32))
+        w_second = keep.tile([P, PACK, HALF], F32, name="w_second", tag="bytes_then_w", align_bytes=64)
+        nc.sync.dma_start(out=w_second[:], in_=w_rows[:, :, half(1)])
+
+        d_picked = keep.tile([P, S], U32, name="d_picked", align_bytes=64)
+        d_dealt = keep.tile([P, S], U32, name="d_dealt", align_bytes=64)
+        x_picked = keep.tile([P, S], U32, name="x_picked", align_bytes=64)
+        nc.vector.tensor_copy(d_picked[:], d_word_table[:].bitcast(U32).indirect(k1_list[:]))
+        nc.vector.tensor_copy(
+            d_dealt[:].rearrange("p (t c i) -> p c t i", t=PACK, i=4),
+            d_picked[:].rearrange("p (c i t) -> p c t i", t=PACK, i=4),
+        )
+
+        w_signed = keep.tile([P, PACK, HALF], BF16, name="w_signed")
+        for t in range(PACK):
+            nc.scalar.activation(w_signed[:, t, :], w_first[:, t, :], ACT.Copy, scale=gain_sign[:, t : t + 1])
+        w_grouped = keep.tile([P, HALF * PACK], BF16, name="w_grouped0", align_bytes=64)
+        nc.scalar.copy(
+            w_grouped[:].rearrange("p (c i t) -> p c t i", t=PACK, i=4),
+            w_signed[:].rearrange("p t (c i) -> p c t i", i=4),
+        )
+        w_quantised = [quantise("w0", w_grouped)]
+
+        for a in range(2):
+            nc.vector.tensor_copy(x_picked[:, half(a)], x_word_table[:].bitcast(U32).indirect(half_list(offs_list, a)))
+        h_banks = [psum.tile([P, S], F32, name="h_bank%d" % t, tag="bank%d" % t) for t in range(PACK)]
+
+        def first_product(t, a):
+            rows = slice(t * P, (t + 1) * P)
+            x_planes = planes[:, S + a * HALF : S + (a + 1) * HALF]
+            product(h_banks[t][:, half(a)], d_dealt[:, rows], planes[:, rows], x_picked[:, half(a)], x_planes)
+
+        for a in range(2):
+            for t in range(2):
+                first_product(t, a)
+        for t in range(2, PACK):
+            for a in range(2):
+                first_product(t, a)
+
+        w_grouped = keep.tile([P, HALF * PACK], BF16, name="w_grouped1", align_bytes=64)
+        nc.vector.tensor_tensor(
+            w_grouped[:].rearrange("p (c i t) -> p c t i", t=PACK, i=2),
+            w_second[:].rearrange("p t (c i) -> p c t i", i=2),
+            gain_sign[:].unsqueeze(1).unsqueeze(3).to_broadcast([P, HALF // 2, PACK, 2]),
+            ALU.mult,
+        )
+        w_quantised.append(quantise("w1", w_grouped))
+
+        st = keep.tile([P, PACK, S], F32, name="st")
+        h_n1 = [keep.tile([P, S], F32, name="h_n1_%d" % t, tag="fetched%d" % t) for t in range(PACK)]
+
+        def leave_bank(t):
+            if t == VECTOR_TILE:
                 nc.vector.tensor_scalar(h[t][:, 0:S], h_banks[t][:], gain_size[:, t : t + 1], None, ALU.mult)
             else:
                 nc.scalar.activation(h[t][:, 0:S], h_banks[t][:], ACT.Copy, scale=gain_size[:, t : t + 1])
 
-        def fetch_n1(t, on_vector):
-            if on_vector:
+        def fetch_n1(t):
+            if t in (VECTOR_TILE, SHARED_TILE):
                 for a in range(2):
-                    gather(True, h_n1[t][:, a * HALF : (a + 1) * HALF], h[t][:], entries(n1_list, a * HALF, HALF))
+                    gather(t == VECTOR_TILE or a == 0, h_n1[t][:, half(a)], h[t][:], half_list(n1_list, a))
             else:
                 gather(False, h_n1[t][:], h[t][:], n1_list[:])
-
-        def fetch_n1_half(t, a, on_vector):
-            gather(on_vector, h_n1[t][:, a * HALF : (a + 1) * HALF], h[t][:], entries(n1_list, a * HALF, HALF))
 
         def subtract(t):
             nc.vector.tensor_tensor(st[:, t, :], h[t][:, 0:S], h_n1[t][:], ALU.subtract)
 
-        def fetch_n2(a, t, on_vector):
-            if a not in st_n2:
-                st_n2[a] = keep.tile([P, 4, PIECES[a]], F32, name="st_n2_%d" % a, tag=("st_n2", "fetched2", "fetched3")[a])
-            gather(on_vector, st_n2[a][:, t, :], st[:, t, :], entries(n2_list, starts[a], PIECES[a]))
+        leave_bank(0)
+        leave_bank(1)
+        fetch_n1(1)
+        fetch_n1(0)
+        leave_bank(2)
+        leave_bank(3)
+        subtract(0)
+        subtract(1)
+        fetch_n1(3)
+        fetch_n1(2)
+        subtract(3)
+        subtract(2)
 
-        zs = {}
-
-        def larger(a):
-            start, width = starts[a], PIECES[a]
-            z = keep.tile([P, width * 4], BF16, name="z%d" % a, align_bytes=64)
-            zs[a] = z
+        st_n2 = [
+            keep.tile([P, PACK, HALF], F32, name="st_n2_%d" % a, tag=tag) for a, tag in enumerate(("st_n2", "fetched3"))
+        ]
+        for a in range(2):
+            for t in range(PACK):
+                gather(t == N2_VECTOR_TILE, st_n2[a][:, t, :], st[:, t, :], half_list(n2_list, a))
+        h2_banks = {}
+        for a in range(2):
+            z = keep.tile([P, HALF * PACK], BF16, name="z%d" % a, tag="z", align_bytes=64)
             nc.vector.tensor_tensor(
-                z[:].rearrange("p (c i t) -> p c t i", t=4, i=2),
-                st[:, :, start : start + width].rearrange("p t (c i) -> p c t i", i=2),
+                z[:].rearrange("p (c i t) -> p c t i", t=PACK, i=2),
+                st[:, :, half(a)].rearrange("p t (c i) -> p c t i", i=2),
                 st_n2[a][:].rearrange("p t (c i) -> p c t i", i=2),
                 ALU.max,
             )
-
-        def second_product(a):
-            width, z = PIECES[a], zs[a]
-            z_codes = keep.tile([P, width], U32, name="z_codes%d" % a, align_bytes=64)
-            z_scales = keep.tile([P, width], U8, name="z_scales%d" % a, align_bytes=64)
-            nc.vector.quantize_mx(out=z_codes[:].bitcast(FP8X4), scales=z_scales[:], in_=z[:])
-            per_bank = S // width
-            tiles = [psum.tile([P, per_bank, width], F32, name="h2_bank%d_%d" % (a, b)) for b in range(4 // per_bank)]
-            for m in range(4):
+            z_codes, z_scales = quantise("z%d" % a, z)
+            for m in range(PACK):
+                w_codes, w_scales = w_quantised[m // 2]
                 w_cols = slice((m % 2) * P, (m % 2 + 1) * P)
-                banks[a, m] = tiles[m // per_bank][:, m % per_bank, :]
-                nc.tensor.matmul_mx(
-                    out=banks[a, m],
-                    lhsT=w_codes[m // 2][:, w_cols].bitcast(FP8X4),
-                    lhsT_scale=w_scales[m // 2][:, w_cols],
-                    rhs=z_codes[:].bitcast(FP8X4),
-                    rhs_scale=z_scales[:],
-                    start=True,
-                    stop=True,
-                )
+                bank = psum.tile([P, HALF], F32, name="h2_bank%d_%d" % (a, m), tag="bank%d" % (PACK * a + m))
+                product(bank[:], w_codes[:, w_cols], w_scales[:, w_cols], z_codes[:], z_scales[:])
+                h2_banks[a, m] = bank
 
-        def leave_bank2(a, m, on_vector):
-            dst = h2[m][:, starts[a] : starts[a] + PIECES[a]]
-            if on_vector:
-                nc.vector.tensor_copy(dst, banks[a, m])
-            else:
-                nc.scalar.copy(dst, banks[a, m])
-
-        early = {}
-
-        def fetch_n3(m, a):
-            early[m, a] = keep.tile([P, HALF], F32, name="early_n3_%d_%d" % (m, a))
-            gather(True, early[m, a][:], h2[m][:], entries(n3_list, a * HALF, HALF))
-
-        def finish(m, a, form):
-            h2_n4 = keep.tile([P, HALF], F32, name="h2_n4_%d_%d" % (m, a))
-            gather(False, h2_n4[:], h2[m][:], entries(n4_list, a * HALF, HALF), scale=0.75)
-            result = keep.tile([P, HALF], F32, name="result%d_%d" % (m, a))
-            if form == "early":
-                nc.vector.tensor_tensor(result[:], early[m, a][:], h2_n4[:], ALU.add)
-            elif form == "fused":
-                nc.vector.tensor_tensor(result[:], h2[m][:].indirect(entries(n3_list, a * HALF, HALF)), h2_n4[:], ALU.add)
-            else:
-                h2_n3 = keep.tile([P, HALF], F32, name="h2_n3_%d_%d" % (m, a))
-                gather(form[0] == "v", h2_n3[:], h2[m][:], entries(n3_list, a * HALF, HALF))
-                engine = nc.vector if form[1] == "v" else nc.gpsimd
-                engine.tensor_tensor(result[:], h2_n3[:], h2_n4[:], ALU.add)
-            nc.sync.dma_start(out=out[m * P : (m + 1) * P, a * HALF : (a + 1) * HALF], in_=result[:])
-
-        prepare_w(1)
-        leave_bank(0, False)
-        leave_bank(1, False)
-        fetch_n1(1, True)
-        fetch_n1(0, False)
-        leave_bank(2, False)
-        leave_bank(3, False)
-        subtract(1)
-        subtract(0)
-        fetch_n1(2, False)
-        fetch_n1_half(3, 0, True)
-        fetch_n1_half(3, 1, False)
-        subtract(2)
-        subtract(3)
-        for a in range(3):
-            for t in range(4):
-                fetch_n2(a, t, t == 3)
-        for a in range(3):
-            larger(a)
-            second_product(a)
-        for a in range(3):
-            for m in range(4):
-                leave_bank2(a, m, a == 2 and m > 0)
-        fetch_n3(3, 1)
-        for m in range(4):
+        h2 = [keep.tile([P, S], F32, name="h2_%d" % m) for m in range(PACK)]
+        for pair in range(2):
             for a in range(2):
-                finish(m, a, "early" if (m, a) == (3, 1) else "fused")
+                for m in (2 * pair, 2 * pair + 1):
+                    if a == 1 and m > 0:
+                        nc.vector.tensor_copy(h2[m][:, half(a)], h2_banks[a, m][:])
+                    else:
+                        nc.scalar.copy(h2[m][:, half(a)], h2_banks[a, m][:])
+
+        for m in range(PACK):
+            for a in range(2):
+                h2_n4 = keep.tile([P, HALF], F32, name="h2_n4_%d_%d" % (m, a))
+                gather(False, h2_n4[:], h2[m][:], half_list(n4_list, a), scale=0.75)
+                result = keep.tile([P, HALF], F32, name="result%d_%d" % (m, a))
+                nc.vector.tensor_tensor(result[:], h2[m][:].indirect(half_list(n3_list, a)), h2_n4[:], ALU.add)
+                nc.sync.dma_start(out=out[m * P : (m + 1) * P, half(a)], in_=result[:])

from contextlib import ExitStack

import concourse.mybir as mybir

F32 = mybir.dt.float32
BF16 = mybir.dt.bfloat16
I32 = mybir.dt.int32
U32 = mybir.dt.uint32
U16 = mybir.dt.uint16
U8 = mybir.dt.uint8
FP8X4 = mybir.dt.float8_e4m3fn_x4
ALU = mybir.AluOpType
ACT = mybir.ActivationFunctionType

P = 128
PACK = 4
TABLE = 2048
S = 512
HALF = S // 2
SPARE = 8
VECTOR_TILE = 1
SHARED_TILE = 3
N2_VECTOR_TILE = 2
FLOPS = 2 * 2 * 512 * 512 * 512


def tile_picked_hpqhopmxsum_none_p_kernel(
    tc, x_words, x_scales, d_words, d_scales, gn, w1, offs, k1, n1, n2, n3, n4, out
):
    nc = tc.nc
    with ExitStack() as ctx:
        keep = ctx.enter_context(tc.tile_pool(name="keep", bufs=1))
        psum = ctx.enter_context(tc.psum_pool(name="psum", bufs=1))

        def half(a):
            return slice(a * HALF, (a + 1) * HALF)

        def half_list(tile, a):
            return tile[:, a * HALF // 16 : (a + 1) * HALF // 16]

        def load_list(name, src):
            tile = keep.tile([P, S // 16], U16, name=name)
            nc.sync.dma_start(tile[:], src)
            return tile

        def load_scale_table(name, src):
            tile = keep.tile([P, TABLE], U8, name=name, align_bytes=64)
            rows = src[0].bitcast(I32).unsqueeze(1).to_broadcast([16, 8, TABLE // 4])
            nc.sync.dma_start(out=tile[:].bitcast(I32), in_=rows)
            return tile

        def load_word_table(name, src):
            tile = keep.tile([P, TABLE], I32, name=name, align_bytes=64)
            nc.sync.dma_start(out=tile[:], in_=src[0].rearrange("p n t -> p (n t)").bitcast(I32))
            return tile

        def gather(on_vector, dst, window, offsets, scale=1.0):
            if on_vector:
                nc.vector.tensor_copy(dst, window.indirect(offsets))
            else:
                nc.scalar.activation(dst, window.indirect(offsets), ACT.Copy, scale=scale)

        def quantise(name, grouped):
            codes = keep.tile([P, HALF], U32, name=name + "_codes", align_bytes=64)
            scales = keep.tile([P, HALF], U8, name=name + "_scales", align_bytes=64)
            nc.vector.quantize_mx(out=codes[:].bitcast(FP8X4), scales=scales[:], in_=grouped[:])
            return codes, scales

        def product(bank, left_codes, left_scales, right_codes, right_scales):
            nc.tensor.matmul_mx(
                out=bank,
                lhsT=left_codes.bitcast(FP8X4),
                lhsT_scale=left_scales,
                rhs=right_codes.bitcast(FP8X4),
                rhs_scale=right_scales,
                start=True,
                stop=True,
            )

        k1_list = load_list("k1_list", k1)
        d_scale_table = load_scale_table("d_scale_table", d_scales)
        offs_list = load_list("offs_list", offs)
        x_scale_table = load_scale_table("x_scale_table", x_scales)
        gain = keep.tile([P, PACK], F32, name="gain")
        nc.sync.dma_start(out=gain[:], in_=gn.rearrange("(p t) o -> p (t o)", t=PACK))
        w_rows = w1.rearrange("(p t) n -> p t n", t=PACK)
        w_first = keep.tile([P, PACK, HALF], F32, name="w_first")
        nc.sync.dma_start(out=w_first[:], in_=w_rows[:, :, half(0)])
        d_word_table = load_word_table("d_word_table", d_words)
        n1_list = load_list("n1_list", n1)
        n2_list = load_list("n2_list", n2)
        x_word_table = load_word_table("x_word_table", x_words)
        n3_list = load_list("n3_list", n3)
        n4_list = load_list("n4_list", n4)

        planes = keep.tile([P, 2 * S], U8, name="planes", align_bytes=64)
        nc.gpsimd.memset(planes[:].bitcast(I32), 0)
        h = [keep.tile([P, S + SPARE], F32, name="h%d" % t) for t in range(PACK)]
        for tile in h:
            nc.gpsimd.memset(tile[:, S:], 0.0)

        gain_size = keep.tile([P, PACK], F32, name="gain_size")
        nc.scalar.activation(gain_size[:], gain[:], ACT.Abs, scale=0.0625)
        negative = keep.tile([P, PACK], F32, name="negative")
        gain_sign = keep.tile([P, PACK], F32, name="gain_sign")
        nc.gpsimd.tensor_scalar(negative[:], gain[:], 0.0, -2.0, ALU.is_lt, ALU.mult)
        nc.gpsimd.tensor_scalar(gain_sign[:], negative[:], 1.0, 1.0, ALU.mult, ALU.add)

        d_bytes = keep.tile([P, S], U8, name="d_bytes", tag="bytes_then_w", align_bytes=64)
        x_bytes = keep.tile([P, S], U8, name="x_bytes", align_bytes=64)
        both = keep.tile([P, 2 * S], U8, name="both", align_bytes=64)
        nc.vector.tensor_copy(d_bytes[:], d_scale_table[:].indirect(k1_list[:]))
        nc.vector.tensor_copy(x_bytes[:], x_scale_table[:].indirect(offs_list[:]))
        nc.vector.tensor_copy(both[:, S:].bitcast(I32), x_bytes[:].bitcast(I32))
        nc.vector.tensor_copy(
            both[:, 0:S].rearrange("p (t c i) -> p c t i", t=PACK, i=16),
            d_bytes[:].rearrange("p (c i t) -> p c t i", t=PACK, i=16),
        )
        for r in range(4):
            nc.sync.dma_start(out=planes[r:P:32, :].bitcast(I32), in_=both[8 * r : P : 32, :].bitcast(I32))
        w_second = keep.tile([P, PACK, HALF], F32, name="w_second", tag="bytes_then_w", align_bytes=64)
        nc.sync.dma_start(out=w_second[:], in_=w_rows[:, :, half(1)])

        d_picked = keep.tile([P, S], U32, name="d_picked", align_bytes=64)
        d_dealt = keep.tile([P, S], U32, name="d_dealt", align_bytes=64)
        x_picked = keep.tile([P, S], U32, name="x_picked", align_bytes=64)
        nc.vector.tensor_copy(d_picked[:], d_word_table[:].bitcast(U32).indirect(k1_list[:]))
        nc.vector.tensor_copy(
            d_dealt[:].rearrange("p (t c i) -> p c t i", t=PACK, i=4),
            d_picked[:].rearrange("p (c i t) -> p c t i", t=PACK, i=4),
        )

        w_signed = keep.tile([P, PACK, HALF], BF16, name="w_signed")
        for t in range(PACK):
            nc.scalar.activation(w_signed[:, t, :], w_first[:, t, :], ACT.Copy, scale=gain_sign[:, t : t + 1])
        w_grouped = keep.tile([P, HALF * PACK], BF16, name="w_grouped0", align_bytes=64)
        nc.scalar.copy(
            w_grouped[:].rearrange("p (c i t) -> p c t i", t=PACK, i=4),
            w_signed[:].rearrange("p t (c i) -> p c t i", i=4),
        )
        w_quantised = [quantise("w0", w_grouped)]

        for a in range(2):
            nc.vector.tensor_copy(x_picked[:, half(a)], x_word_table[:].bitcast(U32).indirect(half_list(offs_list, a)))
        h_banks = [psum.tile([P, S], F32, name="h_bank%d" % t, tag="bank%d" % t) for t in range(PACK)]

        def first_product(t, a):
            rows = slice(t * P, (t + 1) * P)
            x_planes = planes[:, S + a * HALF : S + (a + 1) * HALF]
            product(h_banks[t][:, half(a)], d_dealt[:, rows], planes[:, rows], x_picked[:, half(a)], x_planes)

        for a in range(2):
            for t in range(2):
                first_product(t, a)
        for t in range(2, PACK):
            for a in range(2):
                first_product(t, a)

        w_grouped = keep.tile([P, HALF * PACK], BF16, name="w_grouped1", align_bytes=64)
        nc.vector.tensor_tensor(
            w_grouped[:].rearrange("p (c i t) -> p c t i", t=PACK, i=2),
            w_second[:].rearrange("p t (c i) -> p c t i", i=2),
            gain_sign[:].unsqueeze(1).unsqueeze(3).to_broadcast([P, HALF // 2, PACK, 2]),
            ALU.mult,
        )
        w_quantised.append(quantise("w1", w_grouped))

        st = keep.tile([P, PACK, S], F32, name="st")
        h_n1 = [keep.tile([P, S], F32, name="h_n1_%d" % t, tag="fetched%d" % t) for t in range(PACK)]

        def leave_bank(t):
            if t == VECTOR_TILE:
                nc.vector.tensor_scalar(h[t][:, 0:S], h_banks[t][:], gain_size[:, t : t + 1], None, ALU.mult)
            else:
                nc.scalar.activation(h[t][:, 0:S], h_banks[t][:], ACT.Copy, scale=gain_size[:, t : t + 1])

        def fetch_n1(t):
            if t in (VECTOR_TILE, SHARED_TILE):
                for a in range(2):
                    gather(t == VECTOR_TILE or a == 0, h_n1[t][:, half(a)], h[t][:], half_list(n1_list, a))
            else:
                gather(False, h_n1[t][:], h[t][:], n1_list[:])

        def subtract(t):
            nc.vector.tensor_tensor(st[:, t, :], h[t][:, 0:S], h_n1[t][:], ALU.subtract)

        leave_bank(0)
        leave_bank(1)
        fetch_n1(1)
        fetch_n1(0)
        leave_bank(2)
        leave_bank(3)
        subtract(0)
        subtract(1)
        fetch_n1(3)
        fetch_n1(2)
        subtract(3)
        subtract(2)

        st_n2 = [
            keep.tile([P, PACK, HALF], F32, name="st_n2_%d" % a, tag=tag) for a, tag in enumerate(("st_n2", "fetched3"))
        ]
        for a in range(2):
            for t in range(PACK):
                gather(t == N2_VECTOR_TILE, st_n2[a][:, t, :], st[:, t, :], half_list(n2_list, a))
        h2_banks = {}
        for a in range(2):
            z = keep.tile([P, HALF * PACK], BF16, name="z%d" % a, tag="z", align_bytes=64)
            nc.vector.tensor_tensor(
                z[:].rearrange("p (c i t) -> p c t i", t=PACK, i=2),
                st[:, :, half(a)].rearrange("p t (c i) -> p c t i", i=2),
                st_n2[a][:].rearrange("p t (c i) -> p c t i", i=2),
                ALU.max,
            )
            z_codes, z_scales = quantise("z%d" % a, z)
            for m in range(PACK):
                w_codes, w_scales = w_quantised[m // 2]
                w_cols = slice((m % 2) * P, (m % 2 + 1) * P)
                bank = psum.tile([P, HALF], F32, name="h2_bank%d_%d" % (a, m), tag="bank%d" % (PACK * a + m))
                product(bank[:], w_codes[:, w_cols], w_scales[:, w_cols], z_codes[:], z_scales[:])
                h2_banks[a, m] = bank

        h2 = [keep.tile([P, S], F32, name="h2_%d" % m) for m in range(PACK)]
        for pair in range(2):
            for a in range(2):
                for m in (2 * pair, 2 * pair + 1):
                    if a == 1 and m > 0:
                        nc.vector.tensor_copy(h2[m][:, half(a)], h2_banks[a, m][:])
                    else:
                        nc.scalar.copy(h2[m][:, half(a)], h2_banks[a, m][:])

        for m in range(PACK):
            for a in range(2):
                h2_n4 = keep.tile([P, HALF], F32, name="h2_n4_%d_%d" % (m, a))
                gather(False, h2_n4[:], h2[m][:], half_list(n4_list, a), scale=0.75)
                result = keep.tile([P, HALF], F32, name="result%d_%d" % (m, a))
                nc.vector.tensor_tensor(result[:], h2[m][:].indirect(half_list(n3_list, a)), h2_n4[:], ALU.add)
                nc.sync.dma_start(out=out[m * P : (m + 1) * P, half(a)], in_=result[:])
